import numpy as np
import ml_dtypes


def mxq(x, axis, fmt="e4m3"):
    dtype, down = {"e4m3": (ml_dtypes.float8_e4m3fn, 7), "e5m2": (ml_dtypes.float8_e5m2, 14)}[fmt]
    v = np.moveaxis(np.asarray(x, np.float32).astype(ml_dtypes.bfloat16).astype(np.float64), axis, -1)
    blocks = v.reshape(v.shape[:-1] + (-1, 32))
    amax = np.abs(blocks).max(-1, keepdims=True)
    byte = np.maximum(np.where(amax > 0, np.frexp(amax)[1] - 1 + 127, 0) - down, 1)
    scale = np.exp2(byte - 127.0)
    codes = (blocks / scale).astype(np.float32).astype(dtype).astype(np.float64)
    return np.moveaxis((codes * scale).reshape(v.shape), -1, axis)


WIDE = False


def mx_kscale(k):
    if not WIDE:
        return np.ones(k)
    levels = np.array([10, -10, 5, -5, 0])
    if k % 512:
        return np.exp2(np.random.permutation(np.resize(levels, k // 32))).repeat(32)
    a = np.empty((k // 512, 16))
    for p in range(k // 512):
        a[p, :8] = np.random.permutation(np.resize(levels, 8))
        for g in range(8):
            far = levels[np.abs(levels - a[p, g]) >= 10]
            a[p, g + 8] = far[np.random.randint(len(far))]
    return np.exp2(a.ravel()).repeat(32)


def f64(x):
    return np.asarray(x).astype(np.float64)


def striped(idx):
    return np.tile(idx.reshape(-1, 16).T, (8, 1)).astype(np.uint16)


def unstriped(offs):
    return offs[:16].T.reshape(-1).astype(np.int64)


def pack_weight(w):
    k, n = w.shape
    w = f64(np.asarray(w, np.float32).astype(ml_dtypes.bfloat16)).reshape(k // 32, 32, n)
    amax = np.abs(w).max(1)
    byte = np.clip(np.where(amax > 0, np.frexp(amax)[1] - 1 + 127 - 7, 1), 1, 254)
    scaled = (w * np.exp2(127.0 - byte)[:, None, :]).reshape(k, n).astype(np.float32)
    words = np.ascontiguousarray(scaled.reshape(k // 512, 128, 4, n).transpose(0, 1, 3, 2)).astype(ml_dtypes.float8_e4m3fn).view(np.uint8)
    return words, np.ascontiguousarray(byte.astype(np.uint8).reshape(k // 512, 16, n))


def unpack_weight(words, scales):
    g, p, n, _ = words.shape
    vals = np.ascontiguousarray(words).view(ml_dtypes.float8_e4m3fn).astype(np.float64) * np.repeat(np.exp2(scales.astype(np.float64) - 127.0), 8, axis=1)[..., None]
    return vals.transpose(0, 1, 3, 2).reshape(g * 512, n)


H, K, T, S, N, D = 512, 1024, 1024, 512, 256, 3
P = 2 ** 7


def setup_inputs():
    n = np.random.standard_normal
    s = mx_kscale(K)[:, None]
    u = mx_kscale(H)
    packed_xT = pack_weight(n((K, T)) * s)
    return {
        "x_words": packed_xT[0],
        "x_scales": packed_xT[1],
        "w1": (n((K, H)) / np.sqrt(K) / s).astype(np.float32),
        "wgt": (np.tile(np.random.uniform(0.1, 0.6, (D, 1, S)), (1, P, 1))).astype(np.float32),
        "unit": (np.random.uniform(0.5, 1.5, (H, 1)) * u[:, None]).astype(np.float32),
        "wo": (n((H, N)) / np.sqrt(H) / u[:, None]).astype(np.float32),
        "offs": striped(np.random.permutation(T)[:S]),
        "pos1": striped(np.random.permutation(S)[:S]),
        "pos2": striped(np.random.permutation(S)[:S]),
        "pos3": striped(np.random.permutation(S)[:S]),
    }


def reference(x_words, x_scales, w1, wgt, unit, wo, offs, pos1, pos2, pos3):
    xq = unpack_weight(x_words, x_scales)[:, unstriped(offs)]
    y = mxq(f64(w1), 0, "e4m3").T @ xq
    mean = y.mean(axis=1, keepdims=True)
    dev = y - mean
    lag = dev[:, unstriped(pos1)] * f64(wgt)[0, :1] + dev[:, unstriped(pos2)] * f64(wgt)[1, :1] + dev[:, unstriped(pos3)] * f64(wgt)[2, :1]
    dev2 = (dev) ** 2
    var = dev2.mean(axis=1, keepdims=True) + 0.05
    locm = (dev * lag) / var
    zz = f64(unit) * locm
    return mxq(f64(wo), 0, "e4m3").T @ mxq(zz, 0, "e4m3")

@@ -1,0 +1,318 @@
+from contextlib import ExitStack
+
+import concourse.mybir as mybir
+from concourse.masks import make_identity
+
+H, K, T, S, N, D = 512, 1024, 1024, 512, 256, 3
+FLOPS = 2 * K * H * S + 2 * H * N * S
+
+F32 = mybir.dt.float32
+BF16 = mybir.dt.bfloat16
+I32 = mybir.dt.int32
+U32 = mybir.dt.uint32
+U16 = mybir.dt.uint16
+U8 = mybir.dt.uint8
+FP8X4 = mybir.dt.float8_e4m3fn_x4
+ACT = mybir.ActivationFunctionType
+ALU = mybir.AluOpType
+
+P = 128
+PACK = 4
+PASSES = K // (P * PACK)
+TILES = H // P
+CHUNKS = S // P
+SPARE = 8
+EPS = 0.05
+
+
+def tile_picked_ymoran_moran_p_kernel(
+    tc, x_words, x_scales, w1, wgt, unit, wo, offs, pos1, pos2, pos3, out
+):
+    nc = tc.nc
+    with ExitStack() as ctx:
+        keep = ctx.enter_context(tc.tile_pool(name="keep", bufs=1))
+        ring = ctx.enter_context(tc.tile_pool(name="ring", bufs=2))
+        psum = ctx.enter_context(tc.psum_pool(name="psum", bufs=2))
+
+        xs_table = keep.tile([P, T], U8, name="xs_table", align_bytes=64)
+        nc.vector.memset(xs_table[:].bitcast(I32), 0)
+        zeros = keep.tile([P, SPARE], F32, name="zeros")
+        nc.vector.memset(zeros[:], 0.0)
+        dev = [keep.tile([P, S + SPARE], F32, name="dev%d" % t) for t in range(TILES)]
+        for t in range(TILES):
+            nc.scalar.activation(dev[t][:, S:], zeros[:], ACT.Square)
+
+        offs_sb = keep.tile([P, S // 16], U16, name="offs_sb")
+        nc.sync.dma_start(offs_sb[:], offs)
+        for q in range(4):
+            nc.sync.dma_start(
+                xs_table[32 * q : 32 * q + 4 * PASSES, :].bitcast(I32),
+                x_scales[:, 4 * q : 4 * q + 4, :].bitcast(I32),
+            )
+        xw_table = [keep.tile([P, T], U32, name="xw_table%d" % g) for g in range(PASSES)]
+        w1_rows = w1.rearrange("(g p j) c -> g p j c", g=PASSES, j=PACK)
+        w1_raw = {}
+
+        def load_x(g):
+            nc.sync.dma_start(
+                xw_table[g][:].bitcast(I32),
+                x_words[g].rearrange("p n t -> p (n t)").bitcast(I32),
+            )
+
+        def load_w1(t, g):
+            w1_raw[t, g] = keep.tile([P, PACK, P], F32, name="w1_raw%d_%d" % (t, g))
+            nc.sync.dma_start(w1_raw[t, g][:], w1_rows[g, :, :, t * P : (t + 1) * P])
+
+        load_x(0)
+        load_w1(0, 0)
+        load_x(1)
+        load_w1(0, 1)
+        load_w1(1, 0)
+        load_w1(1, 1)
+        pos_sb = []
+        wgt_sb = []
+        for d, pos in enumerate((pos1, pos2, pos3)):
+            pos_sb.append(keep.tile([P, S // 16], U16, name="pos_sb%d" % d))
+            nc.sync.dma_start(pos_sb[d][:], pos)
+            wgt_sb.append(keep.tile([P, S], F32, name="wgt_sb%d" % d))
+            nc.sync.dma_start(wgt_sb[d][:], wgt[d])
+        unit_sb = keep.tile([P, TILES, 1], F32, name="unit_sb")
+        with nc.allow_non_contiguous_dma(reason="one value a partition and tile"):
+            nc.sync.dma_start(unit_sb[:], unit.rearrange("(t p) o -> p t o", p=P))
+        for t in range(2, TILES):
+            for g in range(PASSES):
+                load_w1(t, g)
+        wo_raw = keep.tile([P, PACK, N], F32, name="wo_raw")
+        nc.sync.dma_start(wo_raw[:], wo.rearrange("(p j) c -> p j c", j=PACK))
+
+        ident = keep.tile([P, P], F32, name="ident")
+        make_identity(nc, ident[:])
+
+        xs_pick = keep.tile([P, S], U8, name="xs_pick", align_bytes=64)
+        nc.vector.tensor_copy(xs_pick[:], xs_table[:].indirect(offs_sb[:]))
+        xw_pick = [keep.tile([P, S], U32, name="xw_pick%d" % g, align_bytes=64) for g in range(PASSES)]
+
+        def pick_x(g):
+            nc.vector.tensor_copy(xw_pick[g][:], xw_table[g][:].indirect(offs_sb[:]))
+
+        def group(copy, raw, grouped):
+            copy(
+                grouped.rearrange("p (c i j) -> p c j i", i=4, j=PACK),
+                raw[:].rearrange("p j (c i) -> p c j i", i=4),
+            )
+
+        def quantize(flat, name):
+            width = flat.shape[1] // PACK
+            codes = keep.tile([P, width], U32, name=name + "_codes", align_bytes=64)
+            scales = keep.tile([P, width], U8, name=name + "_scales", align_bytes=64)
+            nc.vector.quantize_mx(out=codes[:].bitcast(FP8X4), scales=scales[:], in_=flat)
+            return codes, scales
+
+        def slot(name, t, c0, d, width, dtype):
+            return keep.tile([P, width], dtype, name=name, tag="slot%d_%d_%d" % (t, c0, d), align_bytes=64)
+
+        w1_q = {}
+        W1_SLOT = {2: (0, 0, 2), 3: (1, 0, 1)}
+        y = {}
+
+        def prepare_w1_pass(t, g):
+            grouped = keep.tile([P, P * PACK], BF16, name="w1_grouped%d_%d" % (t, g), align_bytes=64)
+            group(nc.scalar.copy, w1_raw[t, g], grouped[:])
+            codes, scales = quantize(grouped[:], "w1_%d_%d" % (t, g))
+            w1_q[t, g] = codes[:], scales[:]
+
+        def prepare_w1(t):
+            grouped = slot("w1_grouped", *W1_SLOT[t], PASSES * P * PACK, BF16)
+            for g in range(PASSES):
+                group(nc.scalar.copy, w1_raw[t, g], grouped[:, g * P * PACK : (g + 1) * P * PACK])
+            codes, scales = quantize(grouped[:], "w1_%d" % t)
+            for g in range(PASSES):
+                w1_q[t, g] = codes[:, g * P : (g + 1) * P], scales[:, g * P : (g + 1) * P]
+
+        def product_pass(t, g):
+            if g == 0:
+                y[t] = psum.tile([P, S], F32, name="acc")
+            codes, scales = w1_q[t, g]
+            nc.tensor.matmul_mx(
+                out=y[t][:],
+                lhsT=codes.bitcast(FP8X4),
+                lhsT_scale=scales,
+                rhs=xw_pick[g][:].bitcast(FP8X4),
+                rhs_scale=xs_pick[4 * g :, :],
+                start=(g == 0),
+                stop=(g == PASSES - 1),
+            )
+
+        def center(t):
+            unused = ring.tile([P, S], BF16, name="unused")
+            neg_mean = ring.tile([P, 1], F32, name="neg_mean")
+            nc.scalar.activation(unused[:], y[t][:], ACT.Identity, scale=-1.0 / S, accum_out=neg_mean[:])
+            nc.scalar.activation(dev[t][:, :S], y[t][:], ACT.Identity, bias=neg_mean[:])
+
+        inv_var = {}
+        VAR_SLOT = {1: (2, 0, 0), 2: (2, 0, 1), 3: (2, 0, 2)}
+
+        def invert(t, var):
+            inv_var[t] = keep.tile([P, 1], F32, name="inv_var%d" % t)
+            nc.vector.reciprocal(inv_var[t][:], var[:])
+
+        def variance(t):
+            unused = ring.tile([P, S], BF16, name="unused")
+            square_sum = ring.tile([P, 1], F32, name="square_sum")
+            nc.scalar.activation(unused[:], dev[t][:, :S], ACT.Square, accum_out=square_sum[:])
+            var = slot("var", *VAR_SLOT[t], 1, F32)
+            nc.scalar.activation(var[:], square_sum[:], ACT.Identity, scale=1.0 / S, bias=EPS)
+            invert(t, var)
+
+        def center_first():
+            stats = keep.tile([P, 6], F32, name="stats")
+            nc.vector.bn_stats(stats[:], y[0][:])
+            mean_var = keep.tile([P, 2], F32, name="mean_var")
+            nc.vector.bn_aggr(mean_var[:], stats[:])
+            nc.vector.tensor_scalar(dev[0][:, :S], y[0][:], mean_var[:, 0:1], None, ALU.subtract)
+            var = keep.tile([P, 1], F32, name="var0")
+            nc.vector.tensor_scalar(var[:], mean_var[:, 1:2], EPS, None, ALU.add)
+            invert(0, var)
+
+        turned = {}
+        scaled_t = {}
+
+        def scale_and_turn(t):
+            factor = ring.tile([P, 1], F32, name="factor")
+            nc.scalar.activation(factor[:], inv_var[t][:], ACT.Copy, scale=unit_sb[:, t, :])
+            scaled = ring.tile([P, S], F32, name="scaled")
+            nc.scalar.activation(scaled[:], dev[t][:, :S], ACT.Copy, scale=factor[:])
+            turned[t] = psum.tile([P, S], F32, name="turned")
+            for c in range(CHUNKS):
+                nc.tensor.transpose(turned[t][:, c * P : (c + 1) * P], scaled[:, c * P : (c + 1) * P], ident[:])
+
+        def copy_turned(t, c0, c1, dst):
+            nc.scalar.copy(dst[:], turned[t][:, c0 * P : c1 * P])
+            for c in range(c0, c1):
+                scaled_t[t, c] = dst, c - c0
+
+        def gather_lag(t, c0, c1):
+            width = (c1 - c0) * P
+            terms = []
+            for d in range(D):
+                term = slot("term", t, c0, d, width, F32)
+                nc.vector.tensor_tensor(
+                    term[:],
+                    dev[t][:].indirect(pos_sb[d][:, c0 * 8 : c1 * 8]),
+                    wgt_sb[d][:, c0 * P : c1 * P],
+                    ALU.mult,
+                )
+                terms.append(term)
+            lag_t = psum.tile([P, S], F32, name="lag_t")
+            for c in range(c1 - c0):
+                for d in range(D):
+                    nc.tensor.matmul(
+                        lag_t[:, c * P : (c + 1) * P],
+                        lhsT=terms[d][:, c * P : (c + 1) * P],
+                        rhs=ident[:],
+                        is_transpose=True,
+                        start=(d == 0),
+                        stop=(d == D - 1),
+                    )
+            return lag_t
+
+        zz_t = keep.tile([P, CHUNKS, H], BF16, name="zz_t")
+
+        def moran(t, c0, c1, lag_t):
+            src, first = scaled_t[t, c0]
+            nc.vector.tensor_tensor(
+                zz_t[:, c0:c1, t * P : (t + 1) * P],
+                lag_t[:, : (c1 - c0) * P].rearrange("p (c i) -> p c i", i=P),
+                src[:, first * P : (first + c1 - c0) * P].rearrange("p (c i) -> p c i", i=P),
+                ALU.mult,
+            )
+
+        out_rows = out.rearrange("(h m) j -> m h j", m=P)
+
+        def readout(c0, c1, wo_q, copy_out):
+            width = (c1 - c0) * P
+            back = psum.tile([P, 2, 2 * P], F32, name="back")
+            for c in range(c0, c1):
+                words = zz_t[:, c, :].bitcast(F32)
+                for u in range(2):
+                    nc.tensor.transpose(
+                        back[:, u, (c - c0) * P : (c - c0 + 1) * P], words[:, u : H // 2 : 2], ident[:]
+                    )
+            grouped = keep.tile([P, width * PACK], BF16, name="zz_grouped%d" % c0, align_bytes=64)
+            nc.scalar.copy(
+                grouped[:].bitcast(F32).rearrange("p (j u) -> p j u", u=2),
+                back[:, :, :width].rearrange("p u j -> p j u"),
+            )
+            codes, scales = quantize(grouped[:], "zz%d" % c0)
+            acc = psum.tile([P, S], F32, name="acc")
+            for h in range(N // P):
+                nc.tensor.matmul_mx(
+                    out=acc[:, h * width : (h + 1) * width],
+                    lhsT=wo_q[0][:, h * P : (h + 1) * P].bitcast(FP8X4),
+                    lhsT_scale=wo_q[1][:, h * P : (h + 1) * P],
+                    rhs=codes[:].bitcast(FP8X4),
+                    rhs_scale=scales[:],
+                    start=True,
+                    stop=True,
+                )
+            result = keep.tile([P, 2 * width], F32, name="result%d" % c0)
+            copy_out(result[:], acc[:, : 2 * width])
+            nc.sync.dma_start(
+                out_rows[:, :, c0 * P : c1 * P], result[:].rearrange("p (h j) -> p h j", h=2)
+            )
+
+        def products(t):
+            for g in range(PASSES):
+                product_pass(t, g)
+
+        def whole(name):
+            return keep.tile([P, S], F32, name=name)
+
+        pick_x(0)
+        prepare_w1_pass(0, 0)
+        product_pass(0, 0)
+        pick_x(1)
+        prepare_w1_pass(0, 1)
+        product_pass(0, 1)
+        center_first()
+        for g in range(PASSES):
+            prepare_w1_pass(1, g)
+            product_pass(1, g)
+
+        center(1)
+        prepare_w1(2)
+        products(2)
+        lag0 = gather_lag(0, 0, CHUNKS)
+        prepare_w1(3)
+        center(2)
+        products(3)
+        lag1 = gather_lag(1, 0, CHUNKS)
+        scale_and_turn(0)
+        variance(1)
+        center(3)
+        copy_turned(0, 0, CHUNKS, whole("scaled_t0"))
+        moran(0, 0, CHUNKS, lag0)
+        variance(2)
+        variance(3)
+        lag2 = gather_lag(2, 0, CHUNKS)
+        scale_and_turn(1)
+        scale_and_turn(2)
+        copy_turned(1, 0, CHUNKS, whole("scaled_t1"))
+        moran(1, 0, CHUNKS, lag1)
+        lag_a = gather_lag(3, 0, 2)
+        scale_and_turn(3)
+        copy_turned(2, 0, CHUNKS, slot("scaled_t2", 3, 2, 0, S, F32))
+        moran(2, 0, CHUNKS, lag2)
+        copy_turned(3, 0, 2, slot("scaled_t3", 3, 3, 0, 2 * P, F32))
+        copy_turned(3, 2, 4, keep.tile([P, 2 * P], F32, name="scaled_t3b"))
+        wo_grouped = keep.tile([P, N * PACK], BF16, name="wo_grouped", align_bytes=64)
+        group(nc.scalar.copy, wo_raw, wo_grouped[:])
+        wo_q = quantize(wo_grouped[:], "wo")
+        lag_b = gather_lag(3, 2, 3)
+        moran(3, 0, 2, lag_a)
+        lag_c = gather_lag(3, 3, 4)
+        readout(0, 2, wo_q, nc.scalar.copy)
+        moran(3, 2, 3, lag_b)
+        readout(2, 3, wo_q, nc.scalar.copy)
+        moran(3, 3, 4, lag_c)
+        readout(3, 4, wo_q, nc.vector.tensor_copy)

@@ -32,7 +32,7 @@ def tile_picked_ymoran_moran_p_kernel(
     with ExitStack() as ctx:
         keep = ctx.enter_context(tc.tile_pool(name="keep", bufs=1))
         ring = ctx.enter_context(tc.tile_pool(name="ring", bufs=2))
-        psum = ctx.enter_context(tc.psum_pool(name="psum", bufs=2))
+        psum = ctx.enter_context(tc.psum_pool(name="psum", bufs=1))
 
         xs_table = keep.tile([P, T], U8, name="xs_table", align_bytes=64)
         nc.vector.memset(xs_table[:].bitcast(I32), 0)
@@ -45,7 +45,7 @@ def tile_picked_ymoran_moran_p_kernel(
         offs_sb = keep.tile([P, S // 16], U16, name="offs_sb")
         nc.sync.dma_start(offs_sb[:], offs)
         for q in range(4):
-            nc.sync.dma_start(
+            nc.scalar.dma_start(
                 xs_table[32 * q : 32 * q + 4 * PASSES, :].bitcast(I32),
                 x_scales[:, 4 * q : 4 * q + 4, :].bitcast(I32),
             )
@@ -59,16 +59,18 @@ def tile_picked_ymoran_moran_p_kernel(
                 x_words[g].rearrange("p n t -> p (n t)").bitcast(I32),
             )
 
-        def load_w1(t, g):
-            w1_raw[t, g] = keep.tile([P, PACK, P], F32, name="w1_raw%d_%d" % (t, g))
-            nc.sync.dma_start(w1_raw[t, g][:], w1_rows[g, :, :, t * P : (t + 1) * P])
+        def load_w1(t0, t1, g):
+            raw = keep.tile([P, PACK, (t1 - t0) * P], F32, name="w1_raw%d_%d" % (t0, g))
+            nc.sync.dma_start(raw[:], w1_rows[g, :, :, t0 * P : t1 * P])
+            for t in range(t0, t1):
+                w1_raw[t, g] = raw[:, :, (t - t0) * P : (t - t0 + 1) * P]
 
         load_x(0)
-        load_w1(0, 0)
+        load_w1(0, 1, 0)
         load_x(1)
-        load_w1(0, 1)
-        load_w1(1, 0)
-        load_w1(1, 1)
+        load_w1(0, 1, 1)
+        load_w1(1, 2, 0)
+        load_w1(1, 2, 1)
         pos_sb = []
         wgt_sb = []
         for d, pos in enumerate((pos1, pos2, pos3)):
@@ -76,12 +78,11 @@ def tile_picked_ymoran_moran_p_kernel(
             nc.sync.dma_start(pos_sb[d][:], pos)
             wgt_sb.append(keep.tile([P, S], F32, name="wgt_sb%d" % d))
             nc.sync.dma_start(wgt_sb[d][:], wgt[d])
+        for g in range(PASSES):
+            load_w1(2, TILES, g)
         unit_sb = keep.tile([P, TILES, 1], F32, name="unit_sb")
         with nc.allow_non_contiguous_dma(reason="one value a partition and tile"):
             nc.sync.dma_start(unit_sb[:], unit.rearrange("(t p) o -> p t o", p=P))
-        for t in range(2, TILES):
-            for g in range(PASSES):
-                load_w1(t, g)
         wo_raw = keep.tile([P, PACK, N], F32, name="wo_raw")
         nc.sync.dma_start(wo_raw[:], wo.rearrange("(p j) c -> p j c", j=PACK))
 
@@ -98,7 +99,7 @@ def tile_picked_ymoran_moran_p_kernel(
         def group(copy, raw, grouped):
             copy(
                 grouped.rearrange("p (c i j) -> p c j i", i=4, j=PACK),
-                raw[:].rearrange("p j (c i) -> p c j i", i=4),
+                raw.rearrange("p j (c i) -> p c j i", i=4),
             )
 
         def quantize(flat, name):
@@ -108,11 +109,13 @@ def tile_picked_ymoran_moran_p_kernel(
             nc.vector.quantize_mx(out=codes[:].bitcast(FP8X4), scales=scales[:], in_=flat)
             return codes, scales
 
-        def slot(name, t, c0, d, width, dtype):
-            return keep.tile([P, width], dtype, name=name, tag="slot%d_%d_%d" % (t, c0, d), align_bytes=64)
+        def slot(name, tag, width, dtype):
+            return keep.tile([P, width], dtype, name=name, tag=tag, align_bytes=64)
+
+        def bank(name, b):
+            return psum.tile([P, S], F32, name=name, tag="bank%d" % b)
 
         w1_q = {}
-        W1_SLOT = {2: (0, 0, 2), 3: (1, 0, 1)}
         y = {}
 
         def prepare_w1_pass(t, g):
@@ -121,8 +124,8 @@ def tile_picked_ymoran_moran_p_kernel(
             codes, scales = quantize(grouped[:], "w1_%d_%d" % (t, g))
             w1_q[t, g] = codes[:], scales[:]
 
-        def prepare_w1(t):
-            grouped = slot("w1_grouped", *W1_SLOT[t], PASSES * P * PACK, BF16)
+        def prepare_w1(t, tag):
+            grouped = slot("w1_grouped", tag, PASSES * P * PACK, BF16)
             for g in range(PASSES):
                 group(nc.scalar.copy, w1_raw[t, g], grouped[:, g * P * PACK : (g + 1) * P * PACK])
             codes, scales = quantize(grouped[:], "w1_%d" % t)
@@ -131,7 +134,7 @@ def tile_picked_ymoran_moran_p_kernel(
 
         def product_pass(t, g):
             if g == 0:
-                y[t] = psum.tile([P, S], F32, name="acc")
+                y[t] = bank("y", t % 2)
             codes, scales = w1_q[t, g]
             nc.tensor.matmul_mx(
                 out=y[t][:],
@@ -150,19 +153,21 @@ def tile_picked_ymoran_moran_p_kernel(
             nc.scalar.activation(dev[t][:, :S], y[t][:], ACT.Identity, bias=neg_mean[:])
 
         inv_var = {}
-        VAR_SLOT = {1: (2, 0, 0), 2: (2, 0, 1), 3: (2, 0, 2)}
 
-        def invert(t, var):
-            inv_var[t] = keep.tile([P, 1], F32, name="inv_var%d" % t)
-            nc.vector.reciprocal(inv_var[t][:], var[:])
+        def invert(tiles, var):
+            inverse = keep.tile([P, len(tiles)], F32, name="inv_var%d" % tiles[0])
+            nc.vector.reciprocal(inverse[:], var[:])
+            for n, t in enumerate(tiles):
+                inv_var[t] = inverse[:, n : n + 1]
 
-        def variance(t):
-            unused = ring.tile([P, S], BF16, name="unused")
-            square_sum = ring.tile([P, 1], F32, name="square_sum")
-            nc.scalar.activation(unused[:], dev[t][:, :S], ACT.Square, accum_out=square_sum[:])
-            var = slot("var", *VAR_SLOT[t], 1, F32)
+        def variance(tiles, tag):
+            square_sum = keep.tile([P, len(tiles)], F32, name="square_sum%d" % tiles[0])
+            for n, t in enumerate(tiles):
+                unused = ring.tile([P, S], BF16, name="unused")
+                nc.scalar.activation(unused[:], dev[t][:, :S], ACT.Square, accum_out=square_sum[:, n : n + 1])
+            var = slot("var", tag, len(tiles), F32)
             nc.scalar.activation(var[:], square_sum[:], ACT.Identity, scale=1.0 / S, bias=EPS)
-            invert(t, var)
+            invert(tiles, var)
 
         def center_first():
             stats = keep.tile([P, 6], F32, name="stats")
@@ -172,17 +177,17 @@ def tile_picked_ymoran_moran_p_kernel(
             nc.vector.tensor_scalar(dev[0][:, :S], y[0][:], mean_var[:, 0:1], None, ALU.subtract)
             var = keep.tile([P, 1], F32, name="var0")
             nc.vector.tensor_scalar(var[:], mean_var[:, 1:2], EPS, None, ALU.add)
-            invert(0, var)
+            invert((0,), var)
 
         turned = {}
         scaled_t = {}
 
-        def scale_and_turn(t):
-            factor = ring.tile([P, 1], F32, name="factor")
-            nc.scalar.activation(factor[:], inv_var[t][:], ACT.Copy, scale=unit_sb[:, t, :])
-            scaled = ring.tile([P, S], F32, name="scaled")
+        def scale_and_turn(t, b):
+            factor = keep.tile([P, 1], F32, name="factor%d" % t)
+            nc.scalar.activation(factor[:], inv_var[t], ACT.Copy, scale=unit_sb[:, t, :])
+            scaled = keep.tile([P, S], F32, name="scaled%d" % t)
             nc.scalar.activation(scaled[:], dev[t][:, :S], ACT.Copy, scale=factor[:])
-            turned[t] = psum.tile([P, S], F32, name="turned")
+            turned[t] = bank("turned", b)
             for c in range(CHUNKS):
                 nc.tensor.transpose(turned[t][:, c * P : (c + 1) * P], scaled[:, c * P : (c + 1) * P], ident[:])
 
@@ -191,24 +196,29 @@ def tile_picked_ymoran_moran_p_kernel(
             for c in range(c0, c1):
                 scaled_t[t, c] = dst, c - c0
 
-        def gather_lag(t, c0, c1):
-            width = (c1 - c0) * P
-            terms = []
-            for d in range(D):
-                term = slot("term", t, c0, d, width, F32)
+        terms = {}
+
+        def gather(tag, items):
+            run = slot("terms", tag, sum((c1 - c0) * P for t, d, c0, c1 in items), F32)
+            at = 0
+            for t, d, c0, c1 in items:
+                width = (c1 - c0) * P
+                terms[t, d, c0] = run[:, at : at + width]
                 nc.vector.tensor_tensor(
-                    term[:],
+                    terms[t, d, c0],
                     dev[t][:].indirect(pos_sb[d][:, c0 * 8 : c1 * 8]),
                     wgt_sb[d][:, c0 * P : c1 * P],
                     ALU.mult,
                 )
-                terms.append(term)
-            lag_t = psum.tile([P, S], F32, name="lag_t")
+                at = at + width
+
+        def add_turned(t, c0, c1, b):
+            lag_t = bank("lag_t", b)
             for c in range(c1 - c0):
                 for d in range(D):
                     nc.tensor.matmul(
                         lag_t[:, c * P : (c + 1) * P],
-                        lhsT=terms[d][:, c * P : (c + 1) * P],
+                        lhsT=terms[t, d, c0][:, c * P : (c + 1) * P],
                         rhs=ident[:],
                         is_transpose=True,
                         start=(d == 0),
@@ -229,9 +239,9 @@ def tile_picked_ymoran_moran_p_kernel(
 
         out_rows = out.rearrange("(h m) j -> m h j", m=P)
 
-        def readout(c0, c1, wo_q, copy_out):
+        def readout(c0, c1, wo_q, copy_out, b_back, b_out):
             width = (c1 - c0) * P
-            back = psum.tile([P, 2, 2 * P], F32, name="back")
+            back = bank("back", b_back)[:].rearrange("p (u j) -> p u j", u=2)
             for c in range(c0, c1):
                 words = zz_t[:, c, :].bitcast(F32)
                 for u in range(2):
@@ -244,7 +254,7 @@ def tile_picked_ymoran_moran_p_kernel(
                 back[:, :, :width].rearrange("p u j -> p j u"),
             )
             codes, scales = quantize(grouped[:], "zz%d" % c0)
-            acc = psum.tile([P, S], F32, name="acc")
+            acc = bank("acc", b_out)
             for h in range(N // P):
                 nc.tensor.matmul_mx(
                     out=acc[:, h * width : (h + 1) * width],
@@ -279,40 +289,46 @@ def tile_picked_ymoran_moran_p_kernel(
             prepare_w1_pass(1, g)
             product_pass(1, g)
 
+        gather("run0", [(0, 0, 0, 4), (0, 1, 0, 4)])
         center(1)
-        prepare_w1(2)
+        prepare_w1(2, "run1")
         products(2)
-        lag0 = gather_lag(0, 0, CHUNKS)
-        prepare_w1(3)
+        gather("run1", [(0, 2, 0, 4), (1, 0, 0, 4)])
+        scale_and_turn(0, 2)
+        prepare_w1(3, "run2")
+        gather("run2", [(1, 1, 0, 4), (1, 2, 0, 4)])
         center(2)
         products(3)
-        lag1 = gather_lag(1, 0, CHUNKS)
-        scale_and_turn(0)
-        variance(1)
-        center(3)
+        lag0 = add_turned(0, 0, CHUNKS, 3)
+        variance((1,), "run3")
+        gather("run3", [(2, 0, 0, 4), (2, 1, 0, 4)])
         copy_turned(0, 0, CHUNKS, whole("scaled_t0"))
         moran(0, 0, CHUNKS, lag0)
-        variance(2)
-        variance(3)
-        lag2 = gather_lag(2, 0, CHUNKS)
-        scale_and_turn(1)
-        scale_and_turn(2)
-        copy_turned(1, 0, CHUNKS, whole("scaled_t1"))
+        center(3)
+        lag1 = add_turned(1, 0, CHUNKS, 1)
+        variance((2, 3), "run4")
+        gather("run4", [(2, 2, 0, 4), (3, 0, 0, 2), (3, 1, 0, 2), (3, 2, 0, 2)])
+        scale_and_turn(1, 4)
+        scale_and_turn(2, 2)
+        scale_and_turn(3, 5)
+        copy_turned(1, 0, CHUNKS, slot("scaled_t1", "run5", S, F32))
+        lag2 = add_turned(2, 0, CHUNKS, 4)
         moran(1, 0, CHUNKS, lag1)
-        lag_a = gather_lag(3, 0, 2)
-        scale_and_turn(3)
-        copy_turned(2, 0, CHUNKS, slot("scaled_t2", 3, 2, 0, S, F32))
+        gather("run5", [(3, 0, 2, 3), (3, 1, 2, 3), (3, 2, 2, 3)])
+        copy_turned(2, 0, CHUNKS, whole("scaled_t2"))
+        lag_a = add_turned(3, 0, 2, 2)
         moran(2, 0, CHUNKS, lag2)
-        copy_turned(3, 0, 2, slot("scaled_t3", 3, 3, 0, 2 * P, F32))
+        copy_turned(3, 0, 2, slot("scaled_t3", "run6", 2 * P, F32))
         copy_turned(3, 2, 4, keep.tile([P, 2 * P], F32, name="scaled_t3b"))
         wo_grouped = keep.tile([P, N * PACK], BF16, name="wo_grouped", align_bytes=64)
-        group(nc.scalar.copy, wo_raw, wo_grouped[:])
+        group(nc.scalar.copy, wo_raw[:], wo_grouped[:])
         wo_q = quantize(wo_grouped[:], "wo")
-        lag_b = gather_lag(3, 2, 3)
+        lag_b = add_turned(3, 2, 3, 3)
         moran(3, 0, 2, lag_a)
-        lag_c = gather_lag(3, 3, 4)
-        readout(0, 2, wo_q, nc.scalar.copy)
+        gather("run6", [(3, 0, 3, 4), (3, 1, 3, 4), (3, 2, 3, 4)])
+        lag_c = add_turned(3, 3, 4, 0)
+        readout(0, 2, wo_q, nc.scalar.copy, 6, 1)
         moran(3, 2, 3, lag_b)
-        readout(2, 3, wo_q, nc.scalar.copy)
+        readout(2, 3, wo_q, nc.scalar.copy, 7, 4)
         moran(3, 3, 4, lag_c)
-        readout(3, 4, wo_q, nc.vector.tensor_copy)
+        readout(3, 4, wo_q, nc.vector.tensor_copy, 5, 2)

@@ -35,7 +35,9 @@ def tile_picked_ymoran_moran_p_kernel(
         psum = ctx.enter_context(tc.psum_pool(name="psum", bufs=1))
 
         xs_table = keep.tile([P, T], U8, name="xs_table", align_bytes=64)
-        nc.vector.memset(xs_table[:].bitcast(I32), 0)
+        nc.gpsimd.memset(xs_table[:].bitcast(I32), 0)
+        unit_rows = keep.tile([P, P], F32, name="unit_rows")
+        nc.vector.memset(unit_rows[:], 0.0)
         zeros = keep.tile([P, SPARE], F32, name="zeros")
         nc.vector.memset(zeros[:], 0.0)
         dev = [keep.tile([P, S + SPARE], F32, name="dev%d" % t) for t in range(TILES)]
@@ -45,7 +47,7 @@ def tile_picked_ymoran_moran_p_kernel(
         offs_sb = keep.tile([P, S // 16], U16, name="offs_sb")
         nc.sync.dma_start(offs_sb[:], offs)
         for q in range(4):
-            nc.scalar.dma_start(
+            nc.sync.dma_start(
                 xs_table[32 * q : 32 * q + 4 * PASSES, :].bitcast(I32),
                 x_scales[:, 4 * q : 4 * q + 4, :].bitcast(I32),
             )
@@ -60,7 +62,7 @@ def tile_picked_ymoran_moran_p_kernel(
             )
 
         def load_w1(t0, t1, g):
-            raw = keep.tile([P, PACK, (t1 - t0) * P], F32, name="w1_raw%d_%d" % (t0, g))
+            raw = keep.tile([P, PACK, (t1 - t0) * P], F32, name="w1_raw%d_%d" % (t0, g), align_bytes=64)
             nc.sync.dma_start(raw[:], w1_rows[g, :, :, t0 * P : t1 * P])
             for t in range(t0, t1):
                 w1_raw[t, g] = raw[:, :, (t - t0) * P : (t - t0 + 1) * P]
@@ -73,17 +75,22 @@ def tile_picked_ymoran_moran_p_kernel(
         load_w1(1, 2, 1)
         pos_sb = []
         wgt_sb = []
-        for d, pos in enumerate((pos1, pos2, pos3)):
+
+        def load_neighbour(d, pos):
             pos_sb.append(keep.tile([P, S // 16], U16, name="pos_sb%d" % d))
             nc.sync.dma_start(pos_sb[d][:], pos)
             wgt_sb.append(keep.tile([P, S], F32, name="wgt_sb%d" % d))
             nc.sync.dma_start(wgt_sb[d][:], wgt[d])
-        for g in range(PASSES):
-            load_w1(2, TILES, g)
-        unit_sb = keep.tile([P, TILES, 1], F32, name="unit_sb")
-        with nc.allow_non_contiguous_dma(reason="one value a partition and tile"):
-            nc.sync.dma_start(unit_sb[:], unit.rearrange("(t p) o -> p t o", p=P))
-        wo_raw = keep.tile([P, PACK, N], F32, name="wo_raw")
+
+        load_neighbour(0, pos1)
+        load_w1(2, 3, 0)
+        load_w1(2, 3, 1)
+        load_neighbour(1, pos2)
+        load_w1(3, 4, 0)
+        load_w1(3, 4, 1)
+        load_neighbour(2, pos3)
+        nc.sync.dma_start(unit_rows[:TILES, :], unit.rearrange("(t n) o -> t (n o)", n=P))
+        wo_raw = keep.tile([P, PACK, N], F32, name="wo_raw", align_bytes=64)
         nc.sync.dma_start(wo_raw[:], wo.rearrange("(p j) c -> p j c", j=PACK))
 
         ident = keep.tile([P, P], F32, name="ident")
@@ -102,6 +109,12 @@ def tile_picked_ymoran_moran_p_kernel(
                 raw.rearrange("p j (c i) -> p c j i", i=4),
             )
 
+        def group_w1(copy, raw, grouped):
+            copy(
+                grouped.rearrange("p (u l e j) -> p l j u e", u=2, e=2, j=PACK),
+                raw.rearrange("p j (l u e) -> p l j u e", u=2, e=2),
+            )
+
         def quantize(flat, name):
             width = flat.shape[1] // PACK
             codes = keep.tile([P, width], U32, name=name + "_codes", align_bytes=64)
@@ -118,30 +131,28 @@ def tile_picked_ymoran_moran_p_kernel(
         w1_q = {}
         y = {}
 
-        def prepare_w1_pass(t, g):
+        def prepare_w1_pass(t, g, copy):
             grouped = keep.tile([P, P * PACK], BF16, name="w1_grouped%d_%d" % (t, g), align_bytes=64)
-            group(nc.scalar.copy, w1_raw[t, g], grouped[:])
+            group_w1(copy, w1_raw[t, g], grouped[:])
             codes, scales = quantize(grouped[:], "w1_%d_%d" % (t, g))
             w1_q[t, g] = codes[:], scales[:]
 
         def prepare_w1(t, tag):
             grouped = slot("w1_grouped", tag, PASSES * P * PACK, BF16)
             for g in range(PASSES):
-                group(nc.scalar.copy, w1_raw[t, g], grouped[:, g * P * PACK : (g + 1) * P * PACK])
+                group_w1(nc.scalar.copy, w1_raw[t, g], grouped[:, g * P * PACK : (g + 1) * P * PACK])
             codes, scales = quantize(grouped[:], "w1_%d" % t)
             for g in range(PASSES):
                 w1_q[t, g] = codes[:, g * P : (g + 1) * P], scales[:, g * P : (g + 1) * P]
 
-        def product_pass(t, g):
-            if g == 0:
-                y[t] = bank("y", t % 2)
+        def product_pass(t, g, acc, cols):
             codes, scales = w1_q[t, g]
             nc.tensor.matmul_mx(
-                out=y[t][:],
+                out=acc,
                 lhsT=codes.bitcast(FP8X4),
                 lhsT_scale=scales,
-                rhs=xw_pick[g][:].bitcast(FP8X4),
-                rhs_scale=xs_pick[4 * g :, :],
+                rhs=xw_pick[g][:, cols].bitcast(FP8X4),
+                rhs_scale=xs_pick[4 * g :, cols],
                 start=(g == 0),
                 stop=(g == PASSES - 1),
             )
@@ -160,21 +171,25 @@ def tile_picked_ymoran_moran_p_kernel(
             for n, t in enumerate(tiles):
                 inv_var[t] = inverse[:, n : n + 1]
 
-        def variance(tiles, tag):
-            square_sum = keep.tile([P, len(tiles)], F32, name="square_sum%d" % tiles[0])
+        def variance(tiles):
+            square_sum = slot("square_sum", "square_sum%d" % tiles[0], len(tiles), F32)
             for n, t in enumerate(tiles):
                 unused = ring.tile([P, S], BF16, name="unused")
                 nc.scalar.activation(unused[:], dev[t][:, :S], ACT.Square, accum_out=square_sum[:, n : n + 1])
-            var = slot("var", tag, len(tiles), F32)
+            var = slot("var", "var%d" % tiles[0], len(tiles), F32)
             nc.scalar.activation(var[:], square_sum[:], ACT.Identity, scale=1.0 / S, bias=EPS)
             invert(tiles, var)
 
-        def center_first():
-            stats = keep.tile([P, 6], F32, name="stats")
-            nc.vector.bn_stats(stats[:], y[0][:])
+        def center_first(halves):
+            stats = keep.tile([P, 2, 6], F32, name="stats")
+            for n in range(2):
+                nc.vector.bn_stats(stats[:, n, :], halves[n])
             mean_var = keep.tile([P, 2], F32, name="mean_var")
-            nc.vector.bn_aggr(mean_var[:], stats[:])
-            nc.vector.tensor_scalar(dev[0][:, :S], y[0][:], mean_var[:, 0:1], None, ALU.subtract)
+            nc.vector.bn_aggr(mean_var[:], stats[:].rearrange("p n s -> p (n s)"))
+            nc.scalar.activation(dev[0][:, : S // 2], halves[0], ACT.Identity, scale=-1.0, bias=mean_var[:, 0:1])
+            nc.vector.tensor_scalar(
+                dev[0][:, S // 2 : S], halves[1], mean_var[:, 0:1], -1.0, ALU.subtract, ALU.mult
+            )
             var = keep.tile([P, 1], F32, name="var0")
             nc.vector.tensor_scalar(var[:], mean_var[:, 1:2], EPS, None, ALU.add)
             invert((0,), var)
@@ -183,18 +198,17 @@ def tile_picked_ymoran_moran_p_kernel(
         scaled_t = {}
 
         def scale_and_turn(t, b):
-            factor = keep.tile([P, 1], F32, name="factor%d" % t)
-            nc.scalar.activation(factor[:], inv_var[t], ACT.Copy, scale=unit_sb[:, t, :])
-            scaled = keep.tile([P, S], F32, name="scaled%d" % t)
+            factor = slot("factor", "factor%d" % t, 1, F32)
+            nc.scalar.activation(factor[:], inv_var[t], ACT.Copy, scale=unit_sb[:, t : t + 1])
+            scaled = slot("scaled", "scaled%d" % t, S, F32)
             nc.scalar.activation(scaled[:], dev[t][:, :S], ACT.Copy, scale=factor[:])
             turned[t] = bank("turned", b)
             for c in range(CHUNKS):
                 nc.tensor.transpose(turned[t][:, c * P : (c + 1) * P], scaled[:, c * P : (c + 1) * P], ident[:])
 
-        def copy_turned(t, c0, c1, dst):
-            nc.scalar.copy(dst[:], turned[t][:, c0 * P : c1 * P])
-            for c in range(c0, c1):
-                scaled_t[t, c] = dst, c - c0
+        def copy_turned(t):
+            scaled_t[t] = keep.tile([P, S], F32, name="scaled_t%d" % t)
+            nc.scalar.copy(scaled_t[t][:], turned[t][:])
 
         terms = {}
 
@@ -229,11 +243,10 @@ def tile_picked_ymoran_moran_p_kernel(
         zz_t = keep.tile([P, CHUNKS, H], BF16, name="zz_t")
 
         def moran(t, c0, c1, lag_t):
-            src, first = scaled_t[t, c0]
             nc.vector.tensor_tensor(
-                zz_t[:, c0:c1, t * P : (t + 1) * P],
-                lag_t[:, : (c1 - c0) * P].rearrange("p (c i) -> p c i", i=P),
-                src[:, first * P : (first + c1 - c0) * P].rearrange("p (c i) -> p c i", i=P),
+                zz_t[:, c0:c1, :].rearrange("p c (u t r) -> p c u t r", u=2, t=TILES)[:, :, :, t, :],
+                lag_t[:, : (c1 - c0) * P].rearrange("p (c u r) -> p c u r", u=2, r=P // 2),
+                scaled_t[t][:, c0 * P : c1 * P].rearrange("p (c u r) -> p c u r", u=2, r=P // 2),
                 ALU.mult,
             )
 
@@ -246,7 +259,7 @@ def tile_picked_ymoran_moran_p_kernel(
                 words = zz_t[:, c, :].bitcast(F32)
                 for u in range(2):
                     nc.tensor.transpose(
-                        back[:, u, (c - c0) * P : (c - c0 + 1) * P], words[:, u : H // 2 : 2], ident[:]
+                        back[:, u, (c - c0) * P : (c - c0 + 1) * P], words[:, u * P : (u + 1) * P], ident[:]
                     )
             grouped = keep.tile([P, width * PACK], BF16, name="zz_grouped%d" % c0, align_bytes=64)
             nc.scalar.copy(
@@ -271,64 +284,71 @@ def tile_picked_ymoran_moran_p_kernel(
                 out_rows[:, :, c0 * P : c1 * P], result[:].rearrange("p (h j) -> p h j", h=2)
             )
 
-        def products(t):
+        def products(t, b):
+            y[t] = bank("y", b)
             for g in range(PASSES):
-                product_pass(t, g)
+                product_pass(t, g, y[t][:], slice(0, S))
 
-        def whole(name):
-            return keep.tile([P, S], F32, name=name)
+        def half(name):
+            return keep.tile([P, S // 2], F32, name=name)
 
-        pick_x(0)
-        prepare_w1_pass(0, 0)
-        product_pass(0, 0)
-        pick_x(1)
-        prepare_w1_pass(0, 1)
-        product_pass(0, 1)
-        center_first()
+        halves = [bank("y_half", b)[:, : S // 2] for b in (0, 6)]
         for g in range(PASSES):
-            prepare_w1_pass(1, g)
-            product_pass(1, g)
-
-        gather("run0", [(0, 0, 0, 4), (0, 1, 0, 4)])
+            pick_x(g)
+            prepare_w1_pass(0, g, nc.scalar.copy)
+            for n in range(2):
+                product_pass(0, g, halves[n], slice(n * S // 2, (n + 1) * S // 2))
+        center_first(halves)
+        prepare_w1(1, "w1_grouped1")
+        products(1, 1)
+        gather("run0", [(0, 0, 0, 4), (0, 1, 0, 4), (0, 2, 0, 4)])
         center(1)
-        prepare_w1(2, "run1")
-        products(2)
-        gather("run1", [(0, 2, 0, 4), (1, 0, 0, 4)])
-        scale_and_turn(0, 2)
-        prepare_w1(3, "run2")
-        gather("run2", [(1, 1, 0, 4), (1, 2, 0, 4)])
+        prepare_w1(2, "w1_grouped2")
+        products(2, 5)
+        gather("w1_raw2_1", [(1, 0, 0, 4)])
+        prepare_w1(3, "w1_grouped3")
+        products(3, 7)
+        gather("w1_raw3_1", [(1, 1, 0, 4), (1, 2, 0, 4)])
+        dealt = keep.tile([P, P], F32, name="dealt")
+        nc.scalar.copy(
+            dealt[:].rearrange("p (u l e) -> p l u e", u=2, e=2),
+            unit_rows[:].rearrange("p (l u e) -> p l u e", u=2, e=2),
+        )
+        unit_psum = bank("unit_psum", 2)
+        nc.tensor.transpose(unit_psum[:, :P], dealt[:], ident[:])
+        unit_sb = keep.tile([P, TILES], F32, name="unit_sb")
+        nc.scalar.copy(unit_sb[:], unit_psum[:, :TILES])
         center(2)
-        products(3)
-        lag0 = add_turned(0, 0, CHUNKS, 3)
-        variance((1,), "run3")
-        gather("run3", [(2, 0, 0, 4), (2, 1, 0, 4)])
-        copy_turned(0, 0, CHUNKS, whole("scaled_t0"))
-        moran(0, 0, CHUNKS, lag0)
+        variance((1,))
+        gather("square_sum1", [(2, 0, 0, 4), (2, 1, 0, 4), (2, 2, 0, 4)])
         center(3)
-        lag1 = add_turned(1, 0, CHUNKS, 1)
-        variance((2, 3), "run4")
-        gather("run4", [(2, 2, 0, 4), (3, 0, 0, 2), (3, 1, 0, 2), (3, 2, 0, 2)])
-        scale_and_turn(1, 4)
+        scale_and_turn(0, 0)
+        lag0 = add_turned(0, 0, CHUNKS, 3)
+        variance((2, 3))
+        gather("square_sum2", [(3, 0, 0, 2), (3, 1, 0, 2), (3, 2, 0, 2)])
+        scale_and_turn(1, 1)
+        lag1 = add_turned(1, 0, CHUNKS, 6)
+        copy_turned(0)
+        moran(0, 0, CHUNKS, lag0)
         scale_and_turn(2, 2)
-        scale_and_turn(3, 5)
-        copy_turned(1, 0, CHUNKS, slot("scaled_t1", "run5", S, F32))
-        lag2 = add_turned(2, 0, CHUNKS, 4)
+        scale_and_turn(3, 4)
+        copy_turned(1)
         moran(1, 0, CHUNKS, lag1)
-        gather("run5", [(3, 0, 2, 3), (3, 1, 2, 3), (3, 2, 2, 3)])
-        copy_turned(2, 0, CHUNKS, whole("scaled_t2"))
-        lag_a = add_turned(3, 0, 2, 2)
+        lag2 = add_turned(2, 0, CHUNKS, 0)
+        lag3_a = add_turned(3, 0, 2, 1)
+        copy_turned(2)
+        copy_turned(3)
+        gather("factor3", [(3, 0, 2, 3), (3, 1, 2, 3), (3, 2, 2, 3)])
         moran(2, 0, CHUNKS, lag2)
-        copy_turned(3, 0, 2, slot("scaled_t3", "run6", 2 * P, F32))
-        copy_turned(3, 2, 4, keep.tile([P, 2 * P], F32, name="scaled_t3b"))
-        wo_grouped = keep.tile([P, N * PACK], BF16, name="wo_grouped", align_bytes=64)
+        moran(3, 0, 2, lag3_a)
+        wo_grouped = slot("wo_grouped", "scaled3", N * PACK, BF16)
         group(nc.scalar.copy, wo_raw[:], wo_grouped[:])
         wo_q = quantize(wo_grouped[:], "wo")
-        lag_b = add_turned(3, 2, 3, 3)
-        moran(3, 0, 2, lag_a)
-        gather("run6", [(3, 0, 3, 4), (3, 1, 3, 4), (3, 2, 3, 4)])
-        lag_c = add_turned(3, 3, 4, 0)
-        readout(0, 2, wo_q, nc.scalar.copy, 6, 1)
-        moran(3, 2, 3, lag_b)
-        readout(2, 3, wo_q, nc.scalar.copy, 7, 4)
-        moran(3, 3, 4, lag_c)
-        readout(3, 4, wo_q, nc.vector.tensor_copy, 5, 2)
+        gather("square_sum2", [(3, 0, 3, 4), (3, 1, 3, 4), (3, 2, 3, 4)])
+        readout(0, 2, wo_q, nc.scalar.copy, 5, 7)
+        lag3_b = add_turned(3, 2, 3, 3)
+        lag3_c = add_turned(3, 3, 4, 6)
+        moran(3, 2, 3, lag3_b)
+        readout(2, 3, wo_q, nc.scalar.copy, 4, 0)
+        moran(3, 3, 4, lag3_c)
+        readout(3, 4, wo_q, nc.vector.tensor_copy, 2, 1)

@@ -206,8 +206,8 @@ def tile_picked_ymoran_moran_p_kernel(
             for c in range(CHUNKS):
                 nc.tensor.transpose(turned[t][:, c * P : (c + 1) * P], scaled[:, c * P : (c + 1) * P], ident[:])
 
-        def copy_turned(t):
-            scaled_t[t] = keep.tile([P, S], F32, name="scaled_t%d" % t)
+        def copy_turned(t, tag):
+            scaled_t[t] = slot("scaled_t", tag, S, F32)
             nc.scalar.copy(scaled_t[t][:], turned[t][:])
 
         terms = {}
@@ -252,7 +252,7 @@ def tile_picked_ymoran_moran_p_kernel(
 
         out_rows = out.rearrange("(h m) j -> m h j", m=P)
 
-        def readout(c0, c1, wo_q, copy_out, b_back, b_out):
+        def readout(c0, c1, wo_q, b_back, b_out):
             width = (c1 - c0) * P
             back = bank("back", b_back)[:].rearrange("p (u j) -> p u j", u=2)
             for c in range(c0, c1):
@@ -267,10 +267,10 @@ def tile_picked_ymoran_moran_p_kernel(
                 back[:, :, :width].rearrange("p u j -> p j u"),
             )
             codes, scales = quantize(grouped[:], "zz%d" % c0)
-            acc = bank("acc", b_out)
-            for h in range(N // P):
+            for h, copy_out in enumerate((nc.scalar.copy, nc.vector.tensor_copy)):
+                acc = bank("acc", b_out[h])
                 nc.tensor.matmul_mx(
-                    out=acc[:, h * width : (h + 1) * width],
+                    out=acc[:, :width],
                     lhsT=wo_q[0][:, h * P : (h + 1) * P].bitcast(FP8X4),
                     lhsT_scale=wo_q[1][:, h * P : (h + 1) * P],
                     rhs=codes[:].bitcast(FP8X4),
@@ -278,11 +278,9 @@ def tile_picked_ymoran_moran_p_kernel(
                     start=True,
                     stop=True,
                 )
-            result = keep.tile([P, 2 * width], F32, name="result%d" % c0)
-            copy_out(result[:], acc[:, : 2 * width])
-            nc.sync.dma_start(
-                out_rows[:, :, c0 * P : c1 * P], result[:].rearrange("p (h j) -> p h j", h=2)
-            )
+                result = keep.tile([P, width], F32, name="result%d_%d" % (c0, h))
+                copy_out(result[:], acc[:, :width])
+                nc.sync.dma_start(out[h * P : (h + 1) * P, c0 * P : c1 * P], result[:])
 
         def products(t, b):
             y[t] = bank("y", b)
@@ -320,35 +318,38 @@ def tile_picked_ymoran_moran_p_kernel(
         nc.scalar.copy(unit_sb[:], unit_psum[:, :TILES])
         center(2)
         variance((1,))
-        gather("square_sum1", [(2, 0, 0, 4), (2, 1, 0, 4), (2, 2, 0, 4)])
+        gather("square_sum1", [(2, 0, 0, 4), (2, 1, 0, 4)])
         center(3)
         scale_and_turn(0, 0)
         lag0 = add_turned(0, 0, CHUNKS, 3)
         variance((2, 3))
-        gather("square_sum2", [(3, 0, 0, 2), (3, 1, 0, 2), (3, 2, 0, 2)])
+        gather("square_sum2", [(2, 2, 0, 4)])
         scale_and_turn(1, 1)
         lag1 = add_turned(1, 0, CHUNKS, 6)
-        copy_turned(0)
+        copy_turned(0, "var2")
         moran(0, 0, CHUNKS, lag0)
         scale_and_turn(2, 2)
+        gather("factor2", [(3, 0, 0, 2), (3, 1, 0, 2)])
         scale_and_turn(3, 4)
-        copy_turned(1)
+        copy_turned(1, "scaled_t1")
         moran(1, 0, CHUNKS, lag1)
+        gather("factor3", [(3, 2, 0, 2)])
+        gather("scaled3", [(3, 0, 2, 3), (3, 1, 2, 3), (3, 2, 2, 3)])
         lag2 = add_turned(2, 0, CHUNKS, 0)
         lag3_a = add_turned(3, 0, 2, 1)
-        copy_turned(2)
-        copy_turned(3)
-        gather("factor3", [(3, 0, 2, 3), (3, 1, 2, 3), (3, 2, 2, 3)])
+        copy_turned(2, "scaled_t2")
+        copy_turned(3, "scaled_t3")
         moran(2, 0, CHUNKS, lag2)
+        gather("square_sum2", [(3, 0, 3, 4)])
         moran(3, 0, 2, lag3_a)
-        wo_grouped = slot("wo_grouped", "scaled3", N * PACK, BF16)
+        gather("factor2", [(3, 1, 3, 4), (3, 2, 3, 4)])
+        wo_grouped = slot("wo_grouped", "scaled2", N * PACK, BF16)
         group(nc.scalar.copy, wo_raw[:], wo_grouped[:])
         wo_q = quantize(wo_grouped[:], "wo")
-        gather("square_sum2", [(3, 0, 3, 4), (3, 1, 3, 4), (3, 2, 3, 4)])
-        readout(0, 2, wo_q, nc.scalar.copy, 5, 7)
+        readout(0, 2, wo_q, 5, (7, 0))
         lag3_b = add_turned(3, 2, 3, 3)
         lag3_c = add_turned(3, 3, 4, 6)
         moran(3, 2, 3, lag3_b)
-        readout(2, 3, wo_q, nc.scalar.copy, 4, 0)
         moran(3, 3, 4, lag3_c)
-        readout(3, 4, wo_q, nc.vector.tensor_copy, 2, 1)
+        readout(2, 3, wo_q, 4, (1, 5))
+        readout(3, 4, wo_q, 2, (3, 4))

from contextlib import ExitStack

import concourse.mybir as mybir
from concourse.masks import make_identity

H, K, T, S, N, D = 512, 1024, 1024, 512, 256, 3
FLOPS = 2 * K * H * S + 2 * H * N * S

F32 = mybir.dt.float32
BF16 = mybir.dt.bfloat16
I32 = mybir.dt.int32
U32 = mybir.dt.uint32
U16 = mybir.dt.uint16
U8 = mybir.dt.uint8
FP8X4 = mybir.dt.float8_e4m3fn_x4
ACT = mybir.ActivationFunctionType
ALU = mybir.AluOpType

P = 128
PACK = 4
PASSES = K // (P * PACK)
TILES = H // P
CHUNKS = S // P
SPARE = 8
EPS = 0.05


def tile_picked_ymoran_moran_p_kernel(
    tc, x_words, x_scales, w1, wgt, unit, wo, offs, pos1, pos2, pos3, out
):
    nc = tc.nc
    with ExitStack() as ctx:
        keep = ctx.enter_context(tc.tile_pool(name="keep", bufs=1))
        ring = ctx.enter_context(tc.tile_pool(name="ring", bufs=2))
        psum = ctx.enter_context(tc.psum_pool(name="psum", bufs=1))

        xs_table = keep.tile([P, T], U8, name="xs_table", align_bytes=64)
        nc.gpsimd.memset(xs_table[:].bitcast(I32), 0)
        unit_rows = keep.tile([P, P], F32, name="unit_rows")
        nc.vector.memset(unit_rows[:], 0.0)
        zeros = keep.tile([P, SPARE], F32, name="zeros")
        nc.vector.memset(zeros[:], 0.0)
        dev = [keep.tile([P, S + SPARE], F32, name="dev%d" % t) for t in range(TILES)]
        for t in range(TILES):
            nc.scalar.activation(dev[t][:, S:], zeros[:], ACT.Square)

        offs_sb = keep.tile([P, S // 16], U16, name="offs_sb")
        nc.sync.dma_start(offs_sb[:], offs)
        for q in range(4):
            nc.sync.dma_start(
                xs_table[32 * q : 32 * q + 4 * PASSES, :].bitcast(I32),
                x_scales[:, 4 * q : 4 * q + 4, :].bitcast(I32),
            )
        xw_table = [keep.tile([P, T], U32, name="xw_table%d" % g) for g in range(PASSES)]
        w1_rows = w1.rearrange("(g p j) c -> g p j c", g=PASSES, j=PACK)
        w1_raw = {}

        def load_x(g):
            nc.sync.dma_start(
                xw_table[g][:].bitcast(I32),
                x_words[g].rearrange("p n t -> p (n t)").bitcast(I32),
            )

        def load_w1(t0, t1, g):
            raw = keep.tile([P, PACK, (t1 - t0) * P], F32, name="w1_raw%d_%d" % (t0, g), align_bytes=64)
            nc.sync.dma_start(raw[:], w1_rows[g, :, :, t0 * P : t1 * P])
            for t in range(t0, t1):
                w1_raw[t, g] = raw[:, :, (t - t0) * P : (t - t0 + 1) * P]

        load_x(0)
        load_w1(0, 1, 0)
        load_x(1)
        load_w1(0, 1, 1)
        load_w1(1, 2, 0)
        load_w1(1, 2, 1)
        pos_sb = []
        wgt_sb = []

        def load_neighbour(d, pos):
            pos_sb.append(keep.tile([P, S // 16], U16, name="pos_sb%d" % d))
            nc.sync.dma_start(pos_sb[d][:], pos)
            wgt_sb.append(keep.tile([P, S], F32, name="wgt_sb%d" % d))
            nc.sync.dma_start(wgt_sb[d][:], wgt[d])

        load_neighbour(0, pos1)
        load_w1(2, 3, 0)
        load_w1(2, 3, 1)
        load_neighbour(1, pos2)
        load_w1(3, 4, 0)
        load_w1(3, 4, 1)
        load_neighbour(2, pos3)
        nc.sync.dma_start(unit_rows[:TILES, :], unit.rearrange("(t n) o -> t (n o)", n=P))
        wo_raw = keep.tile([P, PACK, N], F32, name="wo_raw", align_bytes=64)
        nc.sync.dma_start(wo_raw[:], wo.rearrange("(p j) c -> p j c", j=PACK))

        ident = keep.tile([P, P], F32, name="ident")
        make_identity(nc, ident[:])

        xs_pick = keep.tile([P, S], U8, name="xs_pick", align_bytes=64)
        nc.vector.tensor_copy(xs_pick[:], xs_table[:].indirect(offs_sb[:]))
        xw_pick = [keep.tile([P, S], U32, name="xw_pick%d" % g, align_bytes=64) for g in range(PASSES)]

        def pick_x(g):
            nc.vector.tensor_copy(xw_pick[g][:], xw_table[g][:].indirect(offs_sb[:]))

        def group(copy, raw, grouped):
            copy(
                grouped.rearrange("p (c i j) -> p c j i", i=4, j=PACK),
                raw.rearrange("p j (c i) -> p c j i", i=4),
            )

        def group_w1(copy, raw, grouped):
            copy(
                grouped.rearrange("p (u l e j) -> p l j u e", u=2, e=2, j=PACK),
                raw.rearrange("p j (l u e) -> p l j u e", u=2, e=2),
            )

        def quantize(flat, name):
            width = flat.shape[1] // PACK
            codes = keep.tile([P, width], U32, name=name + "_codes", align_bytes=64)
            scales = keep.tile([P, width], U8, name=name + "_scales", align_bytes=64)
            nc.vector.quantize_mx(out=codes[:].bitcast(FP8X4), scales=scales[:], in_=flat)
            return codes, scales

        def slot(name, tag, width, dtype):
            return keep.tile([P, width], dtype, name=name, tag=tag, align_bytes=64)

        def bank(name, b):
            return psum.tile([P, S], F32, name=name, tag="bank%d" % b)

        w1_q = {}
        y = {}

        def prepare_w1_pass(t, g, copy):
            grouped = keep.tile([P, P * PACK], BF16, name="w1_grouped%d_%d" % (t, g), align_bytes=64)
            group_w1(copy, w1_raw[t, g], grouped[:])
            codes, scales = quantize(grouped[:], "w1_%d_%d" % (t, g))
            w1_q[t, g] = codes[:], scales[:]

        def prepare_w1(t, tag):
            grouped = slot("w1_grouped", tag, PASSES * P * PACK, BF16)
            for g in range(PASSES):
                group_w1(nc.scalar.copy, w1_raw[t, g], grouped[:, g * P * PACK : (g + 1) * P * PACK])
            codes, scales = quantize(grouped[:], "w1_%d" % t)
            for g in range(PASSES):
                w1_q[t, g] = codes[:, g * P : (g + 1) * P], scales[:, g * P : (g + 1) * P]

        def product_pass(t, g, acc, cols):
            codes, scales = w1_q[t, g]
            nc.tensor.matmul_mx(
                out=acc,
                lhsT=codes.bitcast(FP8X4),
                lhsT_scale=scales,
                rhs=xw_pick[g][:, cols].bitcast(FP8X4),
                rhs_scale=xs_pick[4 * g :, cols],
                start=(g == 0),
                stop=(g == PASSES - 1),
            )

        def center(t):
            unused = ring.tile([P, S], BF16, name="unused")
            neg_mean = ring.tile([P, 1], F32, name="neg_mean")
            nc.scalar.activation(unused[:], y[t][:], ACT.Identity, scale=-1.0 / S, accum_out=neg_mean[:])
            nc.scalar.activation(dev[t][:, :S], y[t][:], ACT.Identity, bias=neg_mean[:])

        inv_var = {}

        def invert(tiles, var):
            inverse = keep.tile([P, len(tiles)], F32, name="inv_var%d" % tiles[0])
            nc.vector.reciprocal(inverse[:], var[:])
            for n, t in enumerate(tiles):
                inv_var[t] = inverse[:, n : n + 1]

        def variance(tiles):
            square_sum = slot("square_sum", "square_sum%d" % tiles[0], len(tiles), F32)
            for n, t in enumerate(tiles):
                unused = ring.tile([P, S], BF16, name="unused")
                nc.scalar.activation(unused[:], dev[t][:, :S], ACT.Square, accum_out=square_sum[:, n : n + 1])
            var = slot("var", "var%d" % tiles[0], len(tiles), F32)
            nc.scalar.activation(var[:], square_sum[:], ACT.Identity, scale=1.0 / S, bias=EPS)
            invert(tiles, var)

        def center_first(halves):
            stats = keep.tile([P, 2, 6], F32, name="stats")
            for n in range(2):
                nc.vector.bn_stats(stats[:, n, :], halves[n])
            mean_var = keep.tile([P, 2], F32, name="mean_var")
            nc.vector.bn_aggr(mean_var[:], stats[:].rearrange("p n s -> p (n s)"))
            nc.scalar.activation(dev[0][:, : S // 2], halves[0], ACT.Identity, scale=-1.0, bias=mean_var[:, 0:1])
            nc.vector.tensor_scalar(
                dev[0][:, S // 2 : S], halves[1], mean_var[:, 0:1], -1.0, ALU.subtract, ALU.mult
            )
            var = keep.tile([P, 1], F32, name="var0")
            nc.vector.tensor_scalar(var[:], mean_var[:, 1:2], EPS, None, ALU.add)
            invert((0,), var)

        turned = {}
        scaled_t = {}

        def scale_and_turn(t, b):
            factor = slot("factor", "factor%d" % t, 1, F32)
            nc.scalar.activation(factor[:], inv_var[t], ACT.Copy, scale=unit_sb[:, t : t + 1])
            scaled = slot("scaled", "scaled%d" % t, S, F32)
            nc.scalar.activation(scaled[:], dev[t][:, :S], ACT.Copy, scale=factor[:])
            turned[t] = bank("turned", b)
            for c in range(CHUNKS):
                nc.tensor.transpose(turned[t][:, c * P : (c + 1) * P], scaled[:, c * P : (c + 1) * P], ident[:])

        def copy_turned(t, tag):
            scaled_t[t] = slot("scaled_t", tag, S, F32)
            nc.scalar.copy(scaled_t[t][:], turned[t][:])

        terms = {}

        def gather(tag, items):
            run = slot("terms", tag, sum((c1 - c0) * P for t, d, c0, c1 in items), F32)
            at = 0
            for t, d, c0, c1 in items:
                width = (c1 - c0) * P
                terms[t, d, c0] = run[:, at : at + width]
                nc.vector.tensor_tensor(
                    terms[t, d, c0],
                    dev[t][:].indirect(pos_sb[d][:, c0 * 8 : c1 * 8]),
                    wgt_sb[d][:, c0 * P : c1 * P],
                    ALU.mult,
                )
                at = at + width

        def add_turned(t, c0, c1, b):
            lag_t = bank("lag_t", b)
            for c in range(c1 - c0):
                for d in range(D):
                    nc.tensor.matmul(
                        lag_t[:, c * P : (c + 1) * P],
                        lhsT=terms[t, d, c0][:, c * P : (c + 1) * P],
                        rhs=ident[:],
                        is_transpose=True,
                        start=(d == 0),
                        stop=(d == D - 1),
                    )
            return lag_t

        zz_t = keep.tile([P, CHUNKS, H], BF16, name="zz_t")

        def moran(t, c0, c1, lag_t):
            nc.vector.tensor_tensor(
                zz_t[:, c0:c1, :].rearrange("p c (u t r) -> p c u t r", u=2, t=TILES)[:, :, :, t, :],
                lag_t[:, : (c1 - c0) * P].rearrange("p (c u r) -> p c u r", u=2, r=P // 2),
                scaled_t[t][:, c0 * P : c1 * P].rearrange("p (c u r) -> p c u r", u=2, r=P // 2),
                ALU.mult,
            )

        out_rows = out.rearrange("(h m) j -> m h j", m=P)

        def readout(c0, c1, wo_q, b_back, b_out):
            width = (c1 - c0) * P
            back = bank("back", b_back)[:].rearrange("p (u j) -> p u j", u=2)
            for c in range(c0, c1):
                words = zz_t[:, c, :].bitcast(F32)
                for u in range(2):
                    nc.tensor.transpose(
                        back[:, u, (c - c0) * P : (c - c0 + 1) * P], words[:, u * P : (u + 1) * P], ident[:]
                    )
            grouped = keep.tile([P, width * PACK], BF16, name="zz_grouped%d" % c0, align_bytes=64)
            nc.scalar.copy(
                grouped[:].bitcast(F32).rearrange("p (j u) -> p j u", u=2),
                back[:, :, :width].rearrange("p u j -> p j u"),
            )
            codes, scales = quantize(grouped[:], "zz%d" % c0)
            for h, copy_out in enumerate((nc.scalar.copy, nc.vector.tensor_copy)):
                acc = bank("acc", b_out[h])
                nc.tensor.matmul_mx(
                    out=acc[:, :width],
                    lhsT=wo_q[0][:, h * P : (h + 1) * P].bitcast(FP8X4),
                    lhsT_scale=wo_q[1][:, h * P : (h + 1) * P],
                    rhs=codes[:].bitcast(FP8X4),
                    rhs_scale=scales[:],
                    start=True,
                    stop=True,
                )
                result = keep.tile([P, width], F32, name="result%d_%d" % (c0, h))
                copy_out(result[:], acc[:, :width])
                nc.sync.dma_start(out[h * P : (h + 1) * P, c0 * P : c1 * P], result[:])

        def products(t, b):
            y[t] = bank("y", b)
            for g in range(PASSES):
                product_pass(t, g, y[t][:], slice(0, S))

        def half(name):
            return keep.tile([P, S // 2], F32, name=name)

        halves = [bank("y_half", b)[:, : S // 2] for b in (0, 6)]
        for g in range(PASSES):
            pick_x(g)
            prepare_w1_pass(0, g, nc.scalar.copy)
            for n in range(2):
                product_pass(0, g, halves[n], slice(n * S // 2, (n + 1) * S // 2))
        center_first(halves)
        prepare_w1(1, "w1_grouped1")
        products(1, 1)
        gather("run0", [(0, 0, 0, 4), (0, 1, 0, 4), (0, 2, 0, 4)])
        center(1)
        prepare_w1(2, "w1_grouped2")
        products(2, 5)
        gather("w1_raw2_1", [(1, 0, 0, 4)])
        prepare_w1(3, "w1_grouped3")
        products(3, 7)
        gather("w1_raw3_1", [(1, 1, 0, 4), (1, 2, 0, 4)])
        dealt = keep.tile([P, P], F32, name="dealt")
        nc.scalar.copy(
            dealt[:].rearrange("p (u l e) -> p l u e", u=2, e=2),
            unit_rows[:].rearrange("p (l u e) -> p l u e", u=2, e=2),
        )
        unit_psum = bank("unit_psum", 2)
        nc.tensor.transpose(unit_psum[:, :P], dealt[:], ident[:])
        unit_sb = keep.tile([P, TILES], F32, name="unit_sb")
        nc.scalar.copy(unit_sb[:], unit_psum[:, :TILES])
        center(2)
        variance((1,))
        gather("square_sum1", [(2, 0, 0, 4), (2, 1, 0, 4)])
        center(3)
        scale_and_turn(0, 0)
        lag0 = add_turned(0, 0, CHUNKS, 3)
        variance((2, 3))
        gather("square_sum2", [(2, 2, 0, 4)])
        scale_and_turn(1, 1)
        lag1 = add_turned(1, 0, CHUNKS, 6)
        copy_turned(0, "var2")
        moran(0, 0, CHUNKS, lag0)
        scale_and_turn(2, 2)
        gather("factor2", [(3, 0, 0, 2), (3, 1, 0, 2)])
        scale_and_turn(3, 4)
        copy_turned(1, "scaled_t1")
        moran(1, 0, CHUNKS, lag1)
        gather("factor3", [(3, 2, 0, 2)])
        gather("scaled3", [(3, 0, 2, 3), (3, 1, 2, 3), (3, 2, 2, 3)])
        lag2 = add_turned(2, 0, CHUNKS, 0)
        lag3_a = add_turned(3, 0, 2, 1)
        copy_turned(2, "scaled_t2")
        copy_turned(3, "scaled_t3")
        moran(2, 0, CHUNKS, lag2)
        gather("square_sum2", [(3, 0, 3, 4)])
        moran(3, 0, 2, lag3_a)
        gather("factor2", [(3, 1, 3, 4), (3, 2, 3, 4)])
        wo_grouped = slot("wo_grouped", "scaled2", N * PACK, BF16)
        group(nc.scalar.copy, wo_raw[:], wo_grouped[:])
        wo_q = quantize(wo_grouped[:], "wo")
        readout(0, 2, wo_q, 5, (7, 0))
        lag3_b = add_turned(3, 2, 3, 3)
        lag3_c = add_turned(3, 3, 4, 6)
        moran(3, 2, 3, lag3_b)
        moran(3, 3, 4, lag3_c)
        readout(2, 3, wo_q, 4, (1, 5))
        readout(3, 4, wo_q, 2, (3, 4))
